import numpy as np, ml_dtypes
CORES = [34,162,290,418,42,426]
N = 6
TK = 32
def setup_inputs(rng):
    return {"c": rng.standard_normal((N, 128, 128), dtype=np.float32).astype(ml_dtypes.bfloat16), "x": rng.standard_normal((N, 128, TK), dtype=np.float32).astype(ml_dtypes.bfloat16)}
def setup_inputs_big(rng):
    d = setup_inputs(rng)
    for k in ("c", "x"): d[k] = (d[k].astype(np.float32) * 1024.0).astype(d[k].dtype)
    return d
def setup_inputs_small(rng):
    d = setup_inputs(rng)
    for k in ("c", "x"): d[k] = (d[k].astype(np.float32) * (1 / 1024.0)).astype(d[k].dtype)
    return d
def setup_inputs_apart(rng):
    d = setup_inputs(rng)
    f = (10.0 ** rng.permutation(np.linspace(-1.5, 1.5, N))).astype(np.float32).reshape(N, 1, 1)
    for k in ("c", "x"): d[k] = (d[k].astype(np.float32) * f).astype(d[k].dtype)
    return d
def reference(c, x):
    C, X = c.astype(np.float64), x.astype(np.float64)
    y = np.zeros((N, 128, TK))
    for r in range(N):
        for j in range(N):
            y[r] += C[(r - j) % N].T @ X[j]
    return {"y": y.astype(ml_dtypes.bfloat16 if x.dtype != np.float64 else np.float64)}

from concourse.bass import DstId, RemoteDMATransfer
from concourse.mybir import AluOpType

N = 6
P = 128
TK = 32
BW = P + TK

SCRATCH = {
    "blk": ("sbuf", [128, N * BW], "bfloat16"),
    "pout": ("sbuf", [128, N * TK], "bfloat16"),
    "land": ("sbuf", [128, N * TK], "bfloat16"),
    "acc": ("sbuf", [128, N * TK], "float32"),
    "yb": ("sbuf", [128, TK], "bfloat16"),
    "ps_own": ("psum", [128, 512], "float32"),
    "ps_out": ("psum", [128, 512], "float32"),
}
SEMAPHORES = (["ld", "ls", "mo", "mw", "cp", "ad", "fin", "st"]
              + ["b%d" % s for s in range(N)] + ["p%d" % s for s in range(N)])

_CACHE = {}


def _hops(topo, a, b):
    if topo.mates(a, b) or topo.same_plane(a, b):
        return 1
    if topo.rack(topo.host(a)) == topo.rack(topo.host(b)):
        return 2
    return 1 if topo.chip(a) == topo.chip(b) else 2


def _sites(topo, cores):
    n = len(cores)
    rng = range(n)
    ok = [[a == b or topo.may_write(cores[a], cores[b]) for b in rng] for a in rng]
    hop = [[0 if a == b else _hops(topo, cores[a], cores[b]) for b in rng] for a in rng]
    terms = [(k, j) for k in rng for j in rng]
    cand = {(k, j): [m for m in rng if ok[k][m] and ok[j][m] and ok[m][(k + j) % n]] for k, j in terms}
    terms.sort(key=lambda t: (len(cand[t]), t))
    crit = [[0] * n for _ in rng]
    use = [[0] * n for _ in rng]
    par = [[0] * n for _ in rng]
    site = {}
    best = [None, None]

    def cost():
        a = max(sum(1 for m in rng if crit[s][m]) for s in rng)
        o = max(sum(1 for r in rng if par[m][r]) for m in rng)
        f = max(sum(1 for m in rng if use[s][m]) for s in rng)
        w = sum(1 for s in rng for m in rng if use[s][m]) + sum(1 for s in rng for m in rng if par[s][m])
        h = sum(5 * hop[s][m] for s in rng for m in rng if use[s][m]) + sum(hop[s][m] for s in rng for m in rng if par[s][m])
        return (a + o, a, f, w, h)

    def put(k, j, m, d):
        r = (k + j) % n
        for s in {k, j}:
            if s != m:
                use[s][m] += d
                if r != m:
                    crit[s][m] += d
        if r != m:
            par[m][r] += d

    def rec(i):
        c = cost()
        if best[0] is not None and c >= best[0]:
            return
        if i == len(terms):
            best[0] = c
            best[1] = dict(site)
            return
        k, j = terms[i]
        for m in cand[(k, j)]:
            put(k, j, m, 1)
            site[(k, j)] = m
            rec(i + 1)
            put(k, j, m, -1)

    rec(0)
    return best[1]


def _split(topo, cores, src, dsts):
    common = -1
    for d in dsts:
        common &= topo.mask(cores[src], cores[d])
    eng = [e for e in range(16) if (common >> e) & 1]
    per = 1
    while per * 2 * len(dsts) <= len(eng):
        per *= 2
    return [(d, per, sum(1 << e for e in eng[i::len(dsts)][:per])) for i, d in enumerate(dsts)]


def _plan(topo, cores):
    key = tuple(cores)
    if key in _CACHE:
        return _CACHE[key]
    n = len(cores)
    rng = range(n)
    site = _sites(topo, cores)
    need = lambda k, j, m: [s for s in sorted({k, j}) if s != m]
    crit = {s: set() for s in rng}
    use = {s: set() for s in rng}
    for (k, j), m in site.items():
        for s in need(k, j, m):
            use[s].add(m)
            if (k + j) % n != m:
                crit[s].add(m)
    calls1, cnt1, when = {}, {}, {}
    for s in rng:
        calls1[s] = []
        done = 0
        for dsts in (sorted(crit[s]), sorted(use[s] - crit[s])):
            if dsts:
                done += len(dsts)
                tr = _split(topo, cores, s, dsts)
                calls1[s].append(tr)
                for d, per, _m in tr:
                    cnt1[(s, d)] = per
                    when[(s, d)] = done
    avail = lambda t, m: max([when[(s, m)] for s in need(t[0], t[1], m)] + [0])
    own, outs, call2, cnt2, when2 = {}, {}, {}, {}, {}
    for m in rng:
        mine = sorted(t for t, q in site.items() if q == m)
        own[m] = sorted((t for t in mine if sum(t) % n == m), key=lambda t: (avail(t, m), t))
        grp = {}
        for t in mine:
            if sum(t) % n != m:
                grp.setdefault(sum(t) % n, []).append(t)
        order = sorted(grp, key=lambda r: (max(avail(t, m) for t in grp[r]), r))
        outs[m] = [(r, sorted(grp[r], key=lambda t: (avail(t, m), t))) for r in order]
        call2[m] = _split(topo, cores, m, order) if order else []
        for r, per, _m in call2[m]:
            cnt2[(m, r)] = per
            when2[(m, r)] = max(avail(t, m) for r2 in order for t in grp[r2]) + len(order)
    srcs = {r: sorted((m for m in rng if (m, r) in cnt2), key=lambda m: (when2[(m, r)], m)) for r in rng}
    _CACHE[key] = dict(calls1=calls1, cnt1=cnt1, own=own, outs=outs, call2=call2, cnt2=cnt2, srcs=srcs, avail=avail, need=need)
    return _CACHE[key]


def rank_program(g, core, T, topo):
    me = T.rank_of(core)
    if me is None:
        return
    cores = list(T.cores)
    pl = _plan(topo, cores)
    sem = T.sem
    c_of = lambda s: T.blk[:, s * BW:s * BW + P]
    x_of = lambda s: T.blk[:, s * BW + P:(s + 1) * BW]
    slot = lambda buf, i: buf[:, i * TK:(i + 1) * TK]

    def send(transfers, src_of, dst_of, sem_of):
        trs = []
        for i, (d, per, mask) in enumerate(transfers):
            rid, pid = topo.addr(cores[d], core)
            trs.append(RemoteDMATransfer(dst_ids=[DstId(rid=rid, pnc=pid)], dma_engine_mask=mask, remote_sem=sem_of(d),
                                         src=src_of(i, d), dst=dst_of(d)))
        g.remote_dma_fused(trs, local_sem=sem.ls)
        return sum(per for _d, per, _m in transfers)

    g.sync.dma_start(c_of(me), T.c[:, :]).then_inc(sem.ld, 16)
    g.scalar.dma_start(x_of(me), T.x[:, :]).then_inc(sem.ld, 16)

    left = 0
    g.wait_ge(sem.ld, 32)
    own_blk = T.blk[:, me * BW:(me + 1) * BW]
    for tr in pl["calls1"][me]:
        left += send(tr, lambda i, d: own_blk, lambda d: own_blk, lambda d: sem["b%d" % me])
    if pl["call2"][me]:
        g.wait_ge(sem.cp, 1)
        left += send(pl["call2"][me], lambda i, d: slot(T.pout, i), lambda d: slot(T.land, me), lambda d: sem["p%d" % me])
    if left:
        g.wait_ge(sem.ls, left)

    own, outs = pl["own"][me], pl["outs"][me]
    early = [t for t in own if pl["avail"](t, me) == 0]
    late = [t for t in own if pl["avail"](t, me) != 0]
    seq = [("own", t) for t in early]
    for i, (_r, ts) in enumerate(outs):
        seq += [(i, t) for t in ts]
    seq += [("own", t) for t in late]
    seen = set()
    count = {}
    size = {"own": len(own)}
    for i, (_r, ts) in enumerate(outs):
        size[i] = len(ts)
    if seq:
        g.tensor.wait_ge(sem.ld, 32)
    for grp, (k, j) in seq:
        for s in pl["need"](k, j, me):
            if s not in seen:
                seen.add(s)
                g.tensor.wait_ge(sem["b%d" % s], pl["cnt1"][(s, me)])
        count[grp] = count.get(grp, 0) + 1
        out = T.ps_own[:, 0:TK] if grp == "own" else slot(T.ps_out, grp)
        mm = g.tensor.matmul(out, c_of(k), x_of(j), start=(count[grp] == 1), stop=(count[grp] == size[grp]))
        if count[grp] == size[grp]:
            mm.then_inc(sem.mw if grp == "own" else sem.mo, 1)

    if outs:
        g.vector.wait_ge(sem.mo, len(outs))
        g.vector.tensor_copy(T.pout[:, 0:len(outs) * TK], T.ps_out[:, 0:len(outs) * TK]).then_inc(sem.cp, 1)
    ops = []
    if own:
        ops.append((T.ps_own[:, 0:TK], sem.mw, 1))
    for m in pl["srcs"][me]:
        ops.append((slot(T.land, m), sem["p%d" % m], pl["cnt2"][(m, me)]))
    run, s0, v0 = ops[0]
    g.vector.wait_ge(s0, v0)
    if len(ops) == 1:
        g.vector.tensor_copy(T.yb[:, :], run).then_inc(sem.fin, 1)
    for i, (ap, s1, v1) in enumerate(ops[1:]):
        g.vector.wait_ge(s1, v1)
        if i:
            g.vector.wait_ge(sem.ad, i)
        if i == len(ops) - 2:
            g.vector.tensor_tensor(T.yb[:, :], run, ap, AluOpType.add).then_inc(sem.fin, 1)
        else:
            g.vector.tensor_tensor(slot(T.acc, i), run, ap, AluOpType.add).then_inc(sem.ad, 1)
            run = slot(T.acc, i)

    g.sync.wait_ge(sem.fin, 1)
    g.sync.dma_start(T.y[:, :], T.yb[:, :]).then_inc(sem.st, 16)
    g.sync.wait_ge(sem.st, 16)
